import numpy as np
import ml_dtypes


def mxq(x, axis, fmt="e4m3"):
    dtype, down = {"e4m3": (ml_dtypes.float8_e4m3fn, 7), "e5m2": (ml_dtypes.float8_e5m2, 14)}[fmt]
    v = np.moveaxis(np.asarray(x, np.float32).astype(ml_dtypes.bfloat16).astype(np.float64), axis, -1)
    blocks = v.reshape(v.shape[:-1] + (-1, 32))
    amax = np.abs(blocks).max(-1, keepdims=True)
    byte = np.maximum(np.where(amax > 0, np.frexp(amax)[1] - 1 + 127, 0) - down, 1)
    scale = np.exp2(byte - 127.0)
    codes = (blocks / scale).astype(np.float32).astype(dtype).astype(np.float64)
    return np.moveaxis((codes * scale).reshape(v.shape), -1, axis)


WIDE = False


def mx_kscale(k):
    if not WIDE:
        return np.ones(k)
    levels = np.array([10, -10, 5, -5, 0])
    if k % 512:
        return np.exp2(np.random.permutation(np.resize(levels, k // 32))).repeat(32)
    a = np.empty((k // 512, 16))
    for p in range(k // 512):
        a[p, :8] = np.random.permutation(np.resize(levels, 8))
        for g in range(8):
            far = levels[np.abs(levels - a[p, g]) >= 10]
            a[p, g + 8] = far[np.random.randint(len(far))]
    return np.exp2(a.ravel()).repeat(32)


def f64(x):
    return np.asarray(x).astype(np.float64)


def striped(idx):
    return np.tile(np.asarray(idx).reshape(-1, 16).T, (8, 1)).astype(np.uint16)


def unstriped(offs):
    return offs[:16].T.reshape(-1).astype(np.int64)


def striped8(idx):
    return np.asarray(idx).reshape(8, -1, 16).transpose(0, 2, 1).reshape(128, -1).astype(np.uint16)


def unstriped8(offs):
    return offs.reshape(8, 16, -1).transpose(0, 2, 1).reshape(8, -1).astype(np.int64)


def pick8(x, idx, run):
    r = np.arange(len(x))
    return x[r[:, None], idx[r % (8 * run) // run]]


E2M1 = np.array([0.0, 0.5, 1.0, 1.5, 2.0, 3.0, 4.0, 6.0, -0.0, -0.5, -1.0, -1.5, -2.0, -3.0, -4.0, -6.0])


def pack_weight(w, fmt):
    k, n = w.shape
    w = f64(np.asarray(w, np.float32).astype(ml_dtypes.bfloat16)).reshape(k // 32, 32, n)
    amax = np.abs(w).max(1)
    if fmt == "e4m3":
        byte = np.frexp(amax)[1] - 1 + 127 - 7
    else:
        mant, ex = np.frexp(amax / 6.0)
        byte = np.where(mant > 0.5, ex, ex - 1) + 127
    byte = np.clip(np.where(amax > 0, byte, 1), 1, 254)
    scaled = (w * np.exp2(127.0 - byte)[:, None, :]).reshape(k, n).astype(np.float32)
    by_word = np.ascontiguousarray(scaled.reshape(k // 512, 128, 4, n).transpose(0, 1, 3, 2))
    if fmt == "e4m3":
        words = by_word.astype(ml_dtypes.float8_e4m3fn).view(np.uint8)
    else:
        c = by_word.astype(ml_dtypes.float4_e2m1fn).view(np.uint8) & 0xF
        words = (c[..., 0::2] | (c[..., 1::2] << 4)).reshape(k // 512, 128, 2 * n)
    return np.ascontiguousarray(words), np.ascontiguousarray(byte.astype(np.uint8).reshape(k // 512, 16, n))


def unpack_weight(words, scales, fmt):
    g, _, n = scales.shape
    words = np.ascontiguousarray(words).reshape(g, 128, n, -1)
    if fmt == "e4m3":
        vals = words.view(ml_dtypes.float8_e4m3fn).astype(np.float64)
    else:
        nib = np.empty((g, 128, n, 4), np.uint8)
        nib[..., 0::2] = words & 0xF
        nib[..., 1::2] = words >> 4
        vals = E2M1[nib]
    vals = vals * np.repeat(np.exp2(scales.astype(np.float64) - 127.0), 8, axis=1)[..., None]
    return vals.transpose(0, 1, 3, 2).reshape(g * 512, n)


K, J, R, T, Z, M, C, O, N, S, U = 512, 512, 512, 1024, 512, 1024, 1024, 256, 256, 1024, 512


def setup_inputs():
    n = np.random.standard_normal
    idx = np.random.permutation(T)[:J]
    idx2 = np.random.permutation(M)[:J]
    idx3 = np.stack([np.random.permutation(C)[:J] for _ in range(8)])
    idx4 = np.stack([np.random.permutation(J)[:O] for _ in range(8)])
    idx5 = np.random.permutation(S)[:N]
    idx6 = np.stack([np.random.permutation(U)[:O] for _ in range(8)])
    fk = mx_kscale(K)
    fr = mx_kscale(R)
    fz = mx_kscale(Z)
    xtp = pack_weight(n((K, T)) * fk[:, None], "e4m3")
    wp = pack_weight(n((K, R)) * 1 / np.sqrt(K) / fk[:, None] * fr, "e4m3")
    xop = pack_weight(n((Z, M)) / fz[:, None], "e4m3")
    w2p = pack_weight(n((Z, R)) * 1 / np.sqrt(Z) * fz[:, None] * fr, "e2m1")
    vsp = pack_weight(n((R, S)) * 1 / np.sqrt(R) / fr[:, None], "e2m1")
    return {
        "xt_words": xtp[0],
        "xt_scales": xtp[1],
        "w_words": wp[0],
        "w_scales": wp[1],
        "xo_words": xop[0],
        "xo_scales": xop[1],
        "w2_words": w2p[0],
        "w2_scales": w2p[1],
        "sa": (np.random.uniform(0.5, 1.6, (R, 1))).astype(np.float32),
        "vs_words": vsp[0],
        "vs_scales": vsp[1],
        "offs": striped(idx),
        "offs2": striped(idx2),
        "offs3": striped8(idx3),
        "offs4": striped8(idx4),
        "offs5": striped(idx5),
        "offs6": striped8(idx6),
    }


def reference(xt_words, xt_scales, w_words, w_scales, xo_words, xo_scales, w2_words, w2_scales, sa, vs_words, vs_scales, offs, offs2, offs3, offs4, offs5, offs6):
    idx = unstriped(offs)
    idx2 = unstriped(offs2)
    idx3 = unstriped8(offs3)
    idx4 = unstriped8(offs4)
    idx5 = unstriped(offs5)
    idx6 = unstriped8(offs6)
    xtu = unpack_weight(xt_words, xt_scales, "e4m3")
    wu = unpack_weight(w_words, w_scales, "e4m3")
    xou = unpack_weight(xo_words, xo_scales, "e4m3")
    w2u = unpack_weight(w2_words, w2_scales, "e2m1")
    vsu = unpack_weight(vs_words, vs_scales, "e2m1")
    xtidxg = xtu[:, idx]
    a = wu.T @ xtidxg
    xoidx2g = xou[:, idx2]
    b = w2u.T @ xoidx2g
    pw = np.zeros((R, C))
    pw[np.arange(R)[:, None], idx3[np.arange(R) % 512 // 64]] = a
    g1 = pw.reshape(R, O, C // O).sum(axis=2)
    hid = np.abs(g1 - pick8(b, idx4, 64) * f64(sa))
    vsidx5g = vsu[:, idx5]
    hidq = mxq(hid, 0, "e4m3")
    p = vsidx5g.T @ hidq
    m0 = np.zeros((N, U))
    m0[np.arange(N)[:, None], idx6[np.arange(N) % 128 // 16]] = p
    m1 = np.pad(m0, ((0, 0), (1, 0)))[:, :U]
    y = m0 - m1
    return y

@@ -1,0 +1,217 @@
+from contextlib import ExitStack
+
+import concourse.mybir as mybir
+
+F32 = mybir.dt.float32
+BF16 = mybir.dt.bfloat16
+I32 = mybir.dt.int32
+U32 = mybir.dt.uint32
+U16 = mybir.dt.uint16
+U8 = mybir.dt.uint8
+FP8X4 = mybir.dt.float8_e4m3fn_x4
+FP4X4 = mybir.dt.float4_e2m1fn_x4
+ALU = mybir.AluOpType
+COPY = mybir.ActivationFunctionType.Copy
+AX = mybir.AxisListType.X
+
+P = 128
+J, R, T, C, O, N, U = 512, 512, 1024, 1024, 256, 256, 512
+FLOPS = 2 * 512 * 512 * 512 * 2 + 2 * 512 * 256 * 256
+HEAD = 128
+HALF = 128
+
+
+def tile_picked_tokens_plain_two_bucketgap_store_endsteps_kernel(
+    tc, xt_words, xt_scales, w_words, w_scales, xo_words, xo_scales, w2_words, w2_scales, sa,
+    vs_words, vs_scales, offs, offs2, offs3, offs4, offs5, offs6, out,
+):
+    nc = tc.nc
+    with ExitStack() as ctx:
+        sb = ctx.enter_context(tc.tile_pool(name="sb", bufs=1))
+        ps = ctx.enter_context(tc.psum_pool(name="ps", bufs=8))
+
+        def tile(name, shape, dtype, tag=None):
+            return sb.tile(shape, dtype, name=name, tag=tag or name, align_bytes=64)
+
+        def bank():
+            return ps.tile([P, 512], F32, name="bank")
+
+        def load_list(name, src):
+            t = tile(name, list(src.shape), U16)
+            nc.sync.dma_start(t[:], src)
+            return t
+
+        def load_scale_rows(queue, plane, src):
+            rows = src[0].bitcast(I32)
+            for q in range(4):
+                queue.dma_start(plane[32 * q : 32 * q + 4, :].bitcast(I32), rows[4 * q : 4 * q + 4, :])
+
+        def zeroed(engine, name, shape, dtype):
+            t = tile(name, shape, dtype)
+            if dtype == U8:
+                engine.memset(t[:].bitcast(I32), 0)
+            else:
+                engine.memset(t[:], 0.0)
+            return t
+
+        xt_plane = zeroed(nc.vector, "xt_plane", [P, T], U8)
+        w_plane = zeroed(nc.vector, "w_plane", [P, R], U8)
+        boards = [zeroed(nc.vector, "board%d" % i, [P, C], F32) for i in range(2)]
+
+        w_stage = tile("w_stage", [4, 4, R // 4], I32)
+        nc.sync.dma_start(w_stage[:], w_scales[0].bitcast(I32).rearrange("(q i) n -> i q n", i=4))
+        l1 = load_list("l1", offs)
+        xt_w = tile("xt_w", [P, T], I32)
+        nc.sync.dma_start(xt_w[:], xt_words[0].rearrange("p n t -> p (n t)").bitcast(I32))
+        load_scale_rows(nc.sync, xt_plane, xt_scales)
+        w_w = tile("w_w", [P, R], I32)
+        nc.sync.dma_start(w_w[:], w_words[0].rearrange("p n t -> p (n t)").bitcast(I32))
+        l3 = load_list("l3", offs3)
+
+        xo_plane = zeroed(nc.gpsimd, "xo_plane", [P, T], U8)
+        w2_plane = zeroed(nc.gpsimd, "w2_plane", [P, R], U8)
+        vs_plane = zeroed(nc.gpsimd, "vs_plane", [P, T], U8)
+        boards.append(zeroed(nc.gpsimd, "board2", [P, C], F32))
+        pages = [zeroed(nc.gpsimd, "page%d" % i, [P, U], F32) for i in range(2)]
+
+        l2 = load_list("l2", offs2)
+        load_scale_rows(nc.sync, xo_plane, xo_scales)
+        xo_w = tile("xo_w", [P, T], I32)
+        nc.sync.dma_start(xo_w[:], xo_words[0].rearrange("p n t -> p (n t)").bitcast(I32))
+        load_scale_rows(nc.sync, w2_plane, w2_scales)
+        w2_w = tile("w2_w", [P, 2 * R], U8)
+        nc.sync.dma_start(w2_w[:].bitcast(I32), w2_words[0].bitcast(I32))
+        l5 = load_list("l5", offs5)
+        load_scale_rows(nc.sync, vs_plane, vs_scales)
+        vs_w = tile("vs_w", [P, 2 * T], U8)
+        nc.sync.dma_start(vs_w[:].bitcast(I32), vs_words[0].bitcast(I32))
+        sa_t = tile("sa_t", [P, 4], F32)
+        nc.sync.dma_start(sa_t[:], sa.rearrange("(p t) o -> p (t o)", t=4))
+        l4 = load_list("l4", offs4)
+        l6 = load_list("l6", offs6)
+
+        for q in range(4):
+            nc.vector.tensor_copy(out=w_plane[32 * q : 32 * q + 4, :].bitcast(I32), in_=w_stage[:, q, :])
+        w_s = tile("w_s", [P, 4, P], U8)
+        nc.vector.tensor_copy(out=w_s[:], in_=w_plane[:].rearrange("p (m t) -> p t m", t=4))
+        w_c = tile("w_c", [P, 4, P], I32)
+        nc.gpsimd.tensor_copy(out=w_c[:, :1, :], in_=w_w[:].rearrange("p (m t) -> p t m", t=4)[:, :1, :])
+        nc.gpsimd.tensor_copy(out=w_c[:, 1:, :], in_=w_w[:].rearrange("p (m t) -> p t m", t=4)[:, 1:, :])
+        xg_s = tile("xg_s", [P, J], U8, tag="picked_scales")
+        xg_w = tile("xg_w", [P, J], U32, tag="picked_words")
+        for j0, j1 in ((0, HEAD), (HEAD, J)):
+            nc.vector.tensor_copy(out=xg_s[:, j0:j1], in_=xt_plane[:].indirect(l1[:, j0 // 16 : j1 // 16]))
+            nc.vector.tensor_copy(out=xg_w[:, j0:j1], in_=xt_w[:].bitcast(U32).indirect(l1[:, j0 // 16 : j1 // 16]))
+
+        def product_a(dst, t, j0, j1):
+            nc.tensor.matmul_mx(
+                out=dst, lhsT=w_c[:, t, :].bitcast(FP8X4), lhsT_scale=w_s[:, t, :],
+                rhs=xg_w[:, j0:j1].bitcast(FP8X4), rhs_scale=xg_s[:, j0:j1], start=True, stop=True,
+            )
+
+        a = [tile("a%d" % t, [P, J], F32) for t in range(4)]
+        for t in range(3):
+            acc = bank()
+            product_a(acc[:, :HEAD], t, 0, HEAD)
+            nc.scalar.activation(out=a[t][:, :HEAD], in_=acc[:, :HEAD], func=COPY)
+            nc.scalar.activation(out=boards[t][:].indirect(l3[:, : HEAD // 16]), in_=a[t][:, :HEAD], func=COPY)
+        for t in range(4):
+            acc = bank()
+            j0 = HEAD if t < 3 else 0
+            if t < 3:
+                product_a(acc[:, HEAD : 2 * HEAD], t, HEAD, 2 * HEAD)
+                product_a(acc[:, 2 * HEAD :], t, 2 * HEAD, J)
+            else:
+                product_a(acc[:], t, 0, J)
+            nc.vector.tensor_copy(out=a[t][:, j0:], in_=acc[:, j0:])
+
+        og_s = tile("og_s", [P, J], U8, tag="picked_scales")
+        nc.vector.tensor_copy(out=og_s[:], in_=xo_plane[:].indirect(l2[:]))
+        og_w = tile("og_w", [P, J], U32, tag="picked_words")
+        nc.vector.tensor_copy(out=og_w[:], in_=xo_w[:].bitcast(U32).indirect(l2[:]))
+        w2_s = tile("w2_s", [P, 4, P], U8)
+        nc.gpsimd.tensor_copy(out=w2_s[:], in_=w2_plane[:].rearrange("p (m t) -> p t m", t=4))
+        w2_c = tile("w2_c", [P, 4, P, 2], U8)
+        nc.gpsimd.tensor_copy(out=w2_c[:], in_=w2_w[:].rearrange("p (m t e) -> p t m e", t=4, e=2))
+
+        sums = tile("sums", [P, 4, O], F32)
+
+        def scatter_a(t):
+            j0 = HEAD if t < 3 else 0
+            nc.scalar.activation(out=boards[t % 3][:].indirect(l3[:, j0 // 16 :]), in_=a[t][:, j0:], func=COPY)
+
+        def bucket_sums(t, o0, n):
+            nc.vector.tensor_reduce(
+                out=sums[:, t, o0 : o0 + n],
+                in_=boards[t % 3][:, 4 * o0 : 4 * (o0 + n)].rearrange("p (o c) -> p o c", c=4),
+                axis=AX, op=ALU.add,
+            )
+
+        for t in range(3):
+            scatter_a(t)
+        bucket_sums(0, 0, O)
+        scatter_a(3)
+
+        b = [tile("b%d" % t, [P, J], F32) for t in range(4)]
+        for t in range(4):
+            acc = bank()
+            nc.tensor.matmul_mx(
+                out=acc[:], lhsT=w2_c[:, t, :, :].rearrange("p m e -> p (m e)").bitcast(FP4X4), lhsT_scale=w2_s[:, t, :],
+                rhs=og_w[:].bitcast(FP8X4), rhs_scale=og_s[:], start=True, stop=True,
+            )
+            nc.vector.tensor_copy(out=b[t][:], in_=acc[:])
+
+        vg_s = tile("vg_s", [P, N], U8)
+        nc.vector.tensor_copy(out=vg_s[:], in_=vs_plane[:].indirect(l5[:]))
+        vg_w = tile("vg_w", [P, 2 * N], U8)
+        nc.vector.tensor_copy(out=vg_w[:].bitcast(U16), in_=vs_w[:].bitcast(U16).indirect(l5[:]))
+
+        bucket_sums(1, 0, O)
+        bucket_sums(2, 0, O)
+
+        picked = tile("picked", [P, 4, O], F32)
+        gap = tile("gap", [P, 4, O], F32)
+        for h in range(2):
+            o0 = h * HALF
+            cols = slice(o0, o0 + HALF)
+            bucket_sums(3, o0, HALF)
+            for t in range(4):
+                nc.scalar.activation(
+                    out=picked[:, t, cols], in_=b[t][:].indirect(l4[:, o0 // 16 : (o0 + HALF) // 16]),
+                    func=COPY, scale=sa_t[:, t : t + 1],
+                )
+        for h in range(2):
+            o0 = h * HALF
+            cols = slice(o0, o0 + HALF)
+            nc.vector.tensor_tensor(out=gap[:, 0:3, cols], in0=sums[:, 0:3, cols], in1=picked[:, 0:3, cols], op=ALU.subtract)
+            nc.vector.tensor_tensor(out=gap[:, 3, cols], in0=sums[:, 3, cols], in1=picked[:, 3, cols], op=ALU.subtract)
+            hid = tile("hid%d" % h, [P, HALF, 4], BF16)
+            woven = gap[:, :, cols].rearrange("p t o -> p o t")
+            nc.vector.scalar_tensor_tensor(out=hid[:], in0=woven, scalar=-1.0, in1=woven, op0=ALU.mult, op1=ALU.max)
+            hq_w = tile("hq_w%d" % h, [P, HALF], U32)
+            hq_s = tile("hq_s%d" % h, [P, HALF], U8)
+            nc.vector.quantize_mx(out=hq_w[:].bitcast(FP8X4), scales=hq_s[:], in_=hid[:].rearrange("p o t -> p (o t)"))
+            acc = bank()
+            for n in range(2):
+                nc.tensor.matmul_mx(
+                    out=acc[:, n * HALF : (n + 1) * HALF],
+                    lhsT=vg_w[:, 2 * P * n : 2 * P * (n + 1)].bitcast(FP4X4), lhsT_scale=vg_s[:, P * n : P * (n + 1)],
+                    rhs=hq_w[:].bitcast(FP8X4), rhs_scale=hq_s[:], start=True, stop=True,
+                )
+            res = tile("res%d" % h, [P, 2 * HALF], F32)
+            if h == 0:
+                nc.scalar.copy(out=res[:], in_=acc[:, : 2 * HALF])
+            else:
+                nc.vector.tensor_copy(out=res[:], in_=acc[:, : 2 * HALF])
+            for n in range(2):
+                nc.scalar.activation(
+                    out=pages[n][:].indirect(l6[:, o0 // 16 : (o0 + HALF) // 16]),
+                    in_=res[:, n * HALF : (n + 1) * HALF], func=COPY,
+                )
+        for n in range(2):
+            y = tile("y%d" % n, [P, U], F32)
+            nc.vector.tensor_copy(out=y[:, 0:1], in_=pages[n][:, 0:1])
+            nc.vector.tensor_tensor(out=y[:, 1:U // 2], in0=pages[n][:, 1:U // 2], in1=pages[n][:, 0:U // 2 - 1], op=ALU.subtract)
+            nc.sync.dma_start(out[n * P : (n + 1) * P, : U // 2], y[:, : U // 2])
+            nc.vector.tensor_tensor(out=y[:, U // 2 :], in0=pages[n][:, U // 2 :], in1=pages[n][:, U // 2 - 1 : U - 1], op=ALU.subtract)
+            nc.sync.dma_start(out[n * P : (n + 1) * P, U // 2 :], y[:, U // 2 :])

@@ -46,8 +46,8 @@ def tile_picked_tokens_plain_two_bucketgap_store_endsteps_kernel(
             for q in range(4):
                 queue.dma_start(plane[32 * q : 32 * q + 4, :].bitcast(I32), rows[4 * q : 4 * q + 4, :])
 
-        def zeroed(engine, name, shape, dtype):
-            t = tile(name, shape, dtype)
+        def zeroed(engine, name, shape, dtype, tag=None):
+            t = tile(name, shape, dtype, tag)
             if dtype == U8:
                 engine.memset(t[:].bitcast(I32), 0)
             else:
@@ -60,19 +60,18 @@ def tile_picked_tokens_plain_two_bucketgap_store_endsteps_kernel(
 
         w_stage = tile("w_stage", [4, 4, R // 4], I32)
         nc.sync.dma_start(w_stage[:], w_scales[0].bitcast(I32).rearrange("(q i) n -> i q n", i=4))
+        xt_stage = tile("xt_stage", [4, 4, T // 4], I32)
+        nc.sync.dma_start(xt_stage[:], xt_scales[0].bitcast(I32).rearrange("(q i) n -> i q n", i=4))
         l1 = load_list("l1", offs)
         xt_w = tile("xt_w", [P, T], I32)
         nc.sync.dma_start(xt_w[:], xt_words[0].rearrange("p n t -> p (n t)").bitcast(I32))
-        load_scale_rows(nc.sync, xt_plane, xt_scales)
         w_w = tile("w_w", [P, R], I32)
         nc.sync.dma_start(w_w[:], w_words[0].rearrange("p n t -> p (n t)").bitcast(I32))
         l3 = load_list("l3", offs3)
 
         xo_plane = zeroed(nc.gpsimd, "xo_plane", [P, T], U8)
         w2_plane = zeroed(nc.gpsimd, "w2_plane", [P, R], U8)
-        vs_plane = zeroed(nc.gpsimd, "vs_plane", [P, T], U8)
         boards.append(zeroed(nc.gpsimd, "board2", [P, C], F32))
-        pages = [zeroed(nc.gpsimd, "page%d" % i, [P, U], F32) for i in range(2)]
 
         l2 = load_list("l2", offs2)
         load_scale_rows(nc.sync, xo_plane, xo_scales)
@@ -82,7 +81,6 @@ def tile_picked_tokens_plain_two_bucketgap_store_endsteps_kernel(
         w2_w = tile("w2_w", [P, 2 * R], U8)
         nc.sync.dma_start(w2_w[:].bitcast(I32), w2_words[0].bitcast(I32))
         l5 = load_list("l5", offs5)
-        load_scale_rows(nc.sync, vs_plane, vs_scales)
         vs_w = tile("vs_w", [P, 2 * T], U8)
         nc.sync.dma_start(vs_w[:].bitcast(I32), vs_words[0].bitcast(I32))
         sa_t = tile("sa_t", [P, 4], F32)
@@ -90,41 +88,48 @@ def tile_picked_tokens_plain_two_bucketgap_store_endsteps_kernel(
         l4 = load_list("l4", offs4)
         l6 = load_list("l6", offs6)
 
-        for q in range(4):
-            nc.vector.tensor_copy(out=w_plane[32 * q : 32 * q + 4, :].bitcast(I32), in_=w_stage[:, q, :])
+        for plane, stage in ((w_plane, w_stage), (xt_plane, xt_stage)):
+            for q in range(4):
+                nc.vector.tensor_copy(out=plane[32 * q : 32 * q + 4, :].bitcast(I32), in_=stage[:, q, :])
         w_s = tile("w_s", [P, 4, P], U8)
-        nc.vector.tensor_copy(out=w_s[:], in_=w_plane[:].rearrange("p (m t) -> p t m", t=4))
-        w_c = tile("w_c", [P, 4, P], I32)
-        nc.gpsimd.tensor_copy(out=w_c[:, :1, :], in_=w_w[:].rearrange("p (m t) -> p t m", t=4)[:, :1, :])
-        nc.gpsimd.tensor_copy(out=w_c[:, 1:, :], in_=w_w[:].rearrange("p (m t) -> p t m", t=4)[:, 1:, :])
-        xg_s = tile("xg_s", [P, J], U8, tag="picked_scales")
-        xg_w = tile("xg_w", [P, J], U32, tag="picked_words")
-        for j0, j1 in ((0, HEAD), (HEAD, J)):
-            nc.vector.tensor_copy(out=xg_s[:, j0:j1], in_=xt_plane[:].indirect(l1[:, j0 // 16 : j1 // 16]))
-            nc.vector.tensor_copy(out=xg_w[:, j0:j1], in_=xt_w[:].bitcast(U32).indirect(l1[:, j0 // 16 : j1 // 16]))
+        nc.gpsimd.tensor_copy(out=w_s[:], in_=w_plane[:].rearrange("p (m t) -> p t m", t=4))
+        vs_plane = zeroed(nc.gpsimd, "vs_plane", [P, T], U8, "w_plane")
+        load_scale_rows(nc.sync, vs_plane, vs_scales)
+        w_c = tile("w_c", [P, 4, P], U32)
+        nc.scalar.copy(out=w_c[:], in_=w_w[:].bitcast(U32).rearrange("p (m t) -> p t m", t=4))
+        head_s = tile("head_s", [P, HEAD], U8, "picked_scales")
+        rest_s = tile("rest_s", [P, J - HEAD], U8, "w_w")
+        head_w = tile("head_w", [P, HEAD], U32)
+        rest_w = tile("rest_w", [P, J - HEAD], U32, "picked_words")
+        nc.vector.tensor_copy(out=head_s[:], in_=xt_plane[:].indirect(l1[:, : HEAD // 16]))
+        nc.vector.tensor_copy(out=head_w[:], in_=xt_w[:].bitcast(U32).indirect(l1[:, : HEAD // 16]))
+        nc.vector.tensor_copy(out=rest_w[:], in_=xt_w[:].bitcast(U32).indirect(l1[:, HEAD // 16 :]))
+        nc.vector.tensor_copy(out=rest_s[:], in_=xt_plane[:].indirect(l1[:, HEAD // 16 :]))
 
-        def product_a(dst, t, j0, j1):
+        def product_a(acc, t, j0, j1):
+            scale = head_s[:] if j0 == 0 else rest_s[:, j0 - HEAD : j1 - HEAD]
+            words = head_w[:] if j0 == 0 else rest_w[:, j0 - HEAD : j1 - HEAD]
             nc.tensor.matmul_mx(
-                out=dst, lhsT=w_c[:, t, :].bitcast(FP8X4), lhsT_scale=w_s[:, t, :],
-                rhs=xg_w[:, j0:j1].bitcast(FP8X4), rhs_scale=xg_s[:, j0:j1], start=True, stop=True,
+                out=acc[:, j0:j1], lhsT=w_c[:, t, :].bitcast(FP8X4), lhsT_scale=w_s[:, t, :],
+                rhs=words.bitcast(FP8X4), rhs_scale=scale, start=True, stop=True,
             )
 
         a = [tile("a%d" % t, [P, J], F32) for t in range(4)]
         for t in range(3):
             acc = bank()
-            product_a(acc[:, :HEAD], t, 0, HEAD)
+            product_a(acc, t, 0, HEAD)
             nc.scalar.activation(out=a[t][:, :HEAD], in_=acc[:, :HEAD], func=COPY)
             nc.scalar.activation(out=boards[t][:].indirect(l3[:, : HEAD // 16]), in_=a[t][:, :HEAD], func=COPY)
         for t in range(4):
             acc = bank()
             j0 = HEAD if t < 3 else 0
-            if t < 3:
-                product_a(acc[:, HEAD : 2 * HEAD], t, HEAD, 2 * HEAD)
-                product_a(acc[:, 2 * HEAD :], t, 2 * HEAD, J)
-            else:
-                product_a(acc[:], t, 0, J)
+            if t == 3:
+                product_a(acc, t, 0, HEAD)
+            product_a(acc, t, HEAD, 2 * HEAD)
+            product_a(acc, t, 2 * HEAD, J)
             nc.vector.tensor_copy(out=a[t][:, j0:], in_=acc[:, j0:])
 
+        boards.append(zeroed(nc.gpsimd, "board3", [P, C], F32, "xt_w"))
         og_s = tile("og_s", [P, J], U8, tag="picked_scales")
         nc.vector.tensor_copy(out=og_s[:], in_=xo_plane[:].indirect(l2[:]))
         og_w = tile("og_w", [P, J], U32, tag="picked_words")
@@ -134,23 +139,20 @@ def tile_picked_tokens_plain_two_bucketgap_store_endsteps_kernel(
         w2_c = tile("w2_c", [P, 4, P, 2], U8)
         nc.gpsimd.tensor_copy(out=w2_c[:], in_=w2_w[:].rearrange("p (m t e) -> p t m e", t=4, e=2))
 
-        sums = tile("sums", [P, 4, O], F32)
 
         def scatter_a(t):
             j0 = HEAD if t < 3 else 0
-            nc.scalar.activation(out=boards[t % 3][:].indirect(l3[:, j0 // 16 :]), in_=a[t][:, j0:], func=COPY)
+            nc.scalar.activation(out=boards[t][:].indirect(l3[:, j0 // 16 :]), in_=a[t][:, j0:], func=COPY)
 
         def bucket_sums(t, o0, n):
             nc.vector.tensor_reduce(
                 out=sums[:, t, o0 : o0 + n],
-                in_=boards[t % 3][:, 4 * o0 : 4 * (o0 + n)].rearrange("p (o c) -> p o c", c=4),
+                in_=boards[t][:, 4 * o0 : 4 * (o0 + n)].rearrange("p (o c) -> p o c", c=4),
                 axis=AX, op=ALU.add,
             )
 
-        for t in range(3):
+        for t in range(4):
             scatter_a(t)
-        bucket_sums(0, 0, O)
-        scatter_a(3)
 
         b = [tile("b%d" % t, [P, J], F32) for t in range(4)]
         for t in range(4):
@@ -161,16 +163,17 @@ def tile_picked_tokens_plain_two_bucketgap_store_endsteps_kernel(
             )
             nc.vector.tensor_copy(out=b[t][:], in_=acc[:])
 
-        vg_s = tile("vg_s", [P, N], U8)
+        vg_s = tile("vg_s", [P, N], U8, "w_s")
         nc.vector.tensor_copy(out=vg_s[:], in_=vs_plane[:].indirect(l5[:]))
-        vg_w = tile("vg_w", [P, 2 * N], U8)
+        vg_w = tile("vg_w", [P, 2 * N], U8, "w_c")
         nc.vector.tensor_copy(out=vg_w[:].bitcast(U16), in_=vs_w[:].bitcast(U16).indirect(l5[:]))
 
-        bucket_sums(1, 0, O)
-        bucket_sums(2, 0, O)
+        pages = [zeroed(nc.gpsimd, "page%d" % i, [P, U], F32, ("w2_w", "w2_plane")[i]) for i in range(2)]
+        sums = tile("sums", [P, 4, O], F32, "picked_words")
+        for t in range(3):
+            bucket_sums(t, 0, O)
 
         picked = tile("picked", [P, 4, O], F32)
-        gap = tile("gap", [P, 4, O], F32)
         for h in range(2):
             o0 = h * HALF
             cols = slice(o0, o0 + HALF)
@@ -183,11 +186,13 @@ def tile_picked_tokens_plain_two_bucketgap_store_endsteps_kernel(
         for h in range(2):
             o0 = h * HALF
             cols = slice(o0, o0 + HALF)
-            nc.vector.tensor_tensor(out=gap[:, 0:3, cols], in0=sums[:, 0:3, cols], in1=picked[:, 0:3, cols], op=ALU.subtract)
-            nc.vector.tensor_tensor(out=gap[:, 3, cols], in0=sums[:, 3, cols], in1=picked[:, 3, cols], op=ALU.subtract)
+            gap = tile("gap%d" % h, [P, 4, HALF], BF16, ("gap0", "hid0")[h])
+            nc.vector.tensor_tensor(out=gap[:, 0:3, :], in0=sums[:, 0:3, cols], in1=picked[:, 0:3, cols], op=ALU.subtract)
+            nc.vector.tensor_tensor(out=gap[:, 3, :], in0=sums[:, 3, cols], in1=picked[:, 3, cols], op=ALU.subtract)
+            size = tile("size%d" % h, [P, 4, HALF], BF16)
+            nc.vector.scalar_tensor_tensor(out=size[:], in0=gap[:], scalar=-1.0, in1=gap[:], op0=ALU.mult, op1=ALU.max)
             hid = tile("hid%d" % h, [P, HALF, 4], BF16)
-            woven = gap[:, :, cols].rearrange("p t o -> p o t")
-            nc.vector.scalar_tensor_tensor(out=hid[:], in0=woven, scalar=-1.0, in1=woven, op0=ALU.mult, op1=ALU.max)
+            nc.vector.tensor_copy(out=hid[:], in_=size[:].rearrange("p t o -> p o t"))
             hq_w = tile("hq_w%d" % h, [P, HALF], U32)
             hq_s = tile("hq_s%d" % h, [P, HALF], U8)
             nc.vector.quantize_mx(out=hq_w[:].bitcast(FP8X4), scales=hq_s[:], in_=hid[:].rearrange("p o t -> p (o t)"))

@@ -12,6 +12,7 @@ FP8X4 = mybir.dt.float8_e4m3fn_x4
 FP4X4 = mybir.dt.float4_e2m1fn_x4
 ALU = mybir.AluOpType
 COPY = mybir.ActivationFunctionType.Copy
+ABS = mybir.ActivationFunctionType.Abs
 AX = mybir.AxisListType.X
 
 P = 128
@@ -63,6 +64,8 @@ def tile_picked_tokens_plain_two_bucketgap_store_endsteps_kernel(
         xt_stage = tile("xt_stage", [4, 4, T // 4], I32)
         nc.sync.dma_start(xt_stage[:], xt_scales[0].bitcast(I32).rearrange("(q i) n -> i q n", i=4))
         l1 = load_list("l1", offs)
+        w2_w = tile("w2_w", [P, 2 * R], U8)
+        nc.sync.dma_start(w2_w[:].bitcast(I32), w2_words[0].bitcast(I32))
         xt_w = tile("xt_w", [P, T], I32)
         nc.sync.dma_start(xt_w[:], xt_words[0].rearrange("p n t -> p (n t)").bitcast(I32))
         w_w = tile("w_w", [P, R], I32)
@@ -71,15 +74,12 @@ def tile_picked_tokens_plain_two_bucketgap_store_endsteps_kernel(
 
         xo_plane = zeroed(nc.gpsimd, "xo_plane", [P, T], U8)
         w2_plane = zeroed(nc.gpsimd, "w2_plane", [P, R], U8)
-        boards.append(zeroed(nc.gpsimd, "board2", [P, C], F32))
 
         l2 = load_list("l2", offs2)
         load_scale_rows(nc.sync, xo_plane, xo_scales)
         xo_w = tile("xo_w", [P, T], I32)
         nc.sync.dma_start(xo_w[:], xo_words[0].rearrange("p n t -> p (n t)").bitcast(I32))
         load_scale_rows(nc.sync, w2_plane, w2_scales)
-        w2_w = tile("w2_w", [P, 2 * R], U8)
-        nc.sync.dma_start(w2_w[:].bitcast(I32), w2_words[0].bitcast(I32))
         l5 = load_list("l5", offs5)
         vs_w = tile("vs_w", [P, 2 * T], U8)
         nc.sync.dma_start(vs_w[:].bitcast(I32), vs_words[0].bitcast(I32))
@@ -91,53 +91,58 @@ def tile_picked_tokens_plain_two_bucketgap_store_endsteps_kernel(
         for plane, stage in ((w_plane, w_stage), (xt_plane, xt_stage)):
             for q in range(4):
                 nc.vector.tensor_copy(out=plane[32 * q : 32 * q + 4, :].bitcast(I32), in_=stage[:, q, :])
-        w_s = tile("w_s", [P, 4, P], U8)
-        nc.gpsimd.tensor_copy(out=w_s[:], in_=w_plane[:].rearrange("p (m t) -> p t m", t=4))
-        vs_plane = zeroed(nc.gpsimd, "vs_plane", [P, T], U8, "w_plane")
-        load_scale_rows(nc.sync, vs_plane, vs_scales)
-        w_c = tile("w_c", [P, 4, P], U32)
-        nc.scalar.copy(out=w_c[:], in_=w_w[:].bitcast(U32).rearrange("p (m t) -> p t m", t=4))
+        w2_c = tile("w2_c", [P, 4, P], U16)
+        nc.scalar.copy(out=w2_c[:], in_=w2_w[:].bitcast(U16).rearrange("p (m t) -> p t m", t=4))
+        w_s0 = tile("w_s0", [P, P], U8)
+        w_s = tile("w_s", [P, 3, P], U8)
+        nc.vector.tensor_copy(out=w_s0[:], in_=w_plane[:].rearrange("p (m t) -> p t m", t=4)[:, 0, :])
+        w_c0 = tile("w_c0", [P, P], U32)
+        w_c = tile("w_c", [P, 3, P], U32)
+        nc.scalar.copy(out=w_c0[:], in_=w_w[:].bitcast(U32).rearrange("p (m t) -> p t m", t=4)[:, 0, :])
+        nc.scalar.copy(out=w_c[:], in_=w_w[:].bitcast(U32).rearrange("p (m t) -> p t m", t=4)[:, 1:, :])
         head_s = tile("head_s", [P, HEAD], U8, "picked_scales")
-        rest_s = tile("rest_s", [P, J - HEAD], U8, "w_w")
         head_w = tile("head_w", [P, HEAD], U32)
         rest_w = tile("rest_w", [P, J - HEAD], U32, "picked_words")
         nc.vector.tensor_copy(out=head_s[:], in_=xt_plane[:].indirect(l1[:, : HEAD // 16]))
         nc.vector.tensor_copy(out=head_w[:], in_=xt_w[:].bitcast(U32).indirect(l1[:, : HEAD // 16]))
+        nc.vector.tensor_copy(out=w_s[:], in_=w_plane[:].rearrange("p (m t) -> p t m", t=4)[:, 1:, :])
+        board2 = zeroed(nc.gpsimd, "board2", [P, C], F32, "w_plane")
+        boards.append(board2)
         nc.vector.tensor_copy(out=rest_w[:], in_=xt_w[:].bitcast(U32).indirect(l1[:, HEAD // 16 :]))
-        nc.vector.tensor_copy(out=rest_s[:], in_=xt_plane[:].indirect(l1[:, HEAD // 16 :]))
 
-        def product_a(acc, t, j0, j1):
-            scale = head_s[:] if j0 == 0 else rest_s[:, j0 - HEAD : j1 - HEAD]
-            words = head_w[:] if j0 == 0 else rest_w[:, j0 - HEAD : j1 - HEAD]
+        def product_a(dst, t, words, scale):
+            w_codes, w_bytes = (w_c0[:], w_s0[:]) if t == 0 else (w_c[:, t - 1, :], w_s[:, t - 1, :])
             nc.tensor.matmul_mx(
-                out=acc[:, j0:j1], lhsT=w_c[:, t, :].bitcast(FP8X4), lhsT_scale=w_s[:, t, :],
+                out=dst, lhsT=w_codes.bitcast(FP8X4), lhsT_scale=w_bytes,
                 rhs=words.bitcast(FP8X4), rhs_scale=scale, start=True, stop=True,
             )
 
         a = [tile("a%d" % t, [P, J], F32) for t in range(4)]
-        for t in range(3):
-            acc = bank()
-            product_a(acc, t, 0, HEAD)
-            nc.scalar.activation(out=a[t][:, :HEAD], in_=acc[:, :HEAD], func=COPY)
-            nc.scalar.activation(out=boards[t][:].indirect(l3[:, : HEAD // 16]), in_=a[t][:, :HEAD], func=COPY)
         for t in range(4):
             acc = bank()
+            product_a(acc[:, :HEAD], t, head_w[:], head_s[:])
+            if t < 3:
+                nc.scalar.activation(out=a[t][:, :HEAD], in_=acc[:, :HEAD], func=COPY)
+                nc.scalar.activation(out=boards[t][:].indirect(l3[:, : HEAD // 16]), in_=a[t][:, :HEAD], func=COPY)
+        last_acc = acc
+        rest_s = tile("rest_s", [P, J - HEAD], U8, "picked_scales")
+        nc.vector.tensor_copy(out=rest_s[:], in_=xt_plane[:].indirect(l1[:, HEAD // 16 :]))
+        for t in range(4):
+            acc = bank() if t < 3 else last_acc
             j0 = HEAD if t < 3 else 0
-            if t == 3:
-                product_a(acc, t, 0, HEAD)
-            product_a(acc, t, HEAD, 2 * HEAD)
-            product_a(acc, t, 2 * HEAD, J)
+            product_a(acc[:, HEAD : 2 * HEAD], t, rest_w[:, :HEAD], rest_s[:, :HEAD])
+            product_a(acc[:, 2 * HEAD :], t, rest_w[:, HEAD:], rest_s[:, HEAD:])
             nc.vector.tensor_copy(out=a[t][:, j0:], in_=acc[:, j0:])
 
-        boards.append(zeroed(nc.gpsimd, "board3", [P, C], F32, "xt_w"))
+        boards.append(zeroed(nc.gpsimd, "board3", [P, C], F32, "xt_plane"))
+        vs_plane = zeroed(nc.gpsimd, "vs_plane", [P, T], U8, "w_c0")
+        load_scale_rows(nc.sync, vs_plane, vs_scales)
         og_s = tile("og_s", [P, J], U8, tag="picked_scales")
         nc.vector.tensor_copy(out=og_s[:], in_=xo_plane[:].indirect(l2[:]))
         og_w = tile("og_w", [P, J], U32, tag="picked_words")
         nc.vector.tensor_copy(out=og_w[:], in_=xo_w[:].bitcast(U32).indirect(l2[:]))
-        w2_s = tile("w2_s", [P, 4, P], U8)
-        nc.gpsimd.tensor_copy(out=w2_s[:], in_=w2_plane[:].rearrange("p (m t) -> p t m", t=4))
-        w2_c = tile("w2_c", [P, 4, P, 2], U8)
-        nc.gpsimd.tensor_copy(out=w2_c[:], in_=w2_w[:].rearrange("p (m t e) -> p t m e", t=4, e=2))
+        w2_s = tile("w2_s", [P, 4, P], U8, "w_s0")
+        nc.vector.tensor_copy(out=w2_s[:], in_=w2_plane[:].rearrange("p (m t) -> p t m", t=4))
 
 
         def scatter_a(t):
@@ -158,7 +163,7 @@ def tile_picked_tokens_plain_two_bucketgap_store_endsteps_kernel(
         for t in range(4):
             acc = bank()
             nc.tensor.matmul_mx(
-                out=acc[:], lhsT=w2_c[:, t, :, :].rearrange("p m e -> p (m e)").bitcast(FP4X4), lhsT_scale=w2_s[:, t, :],
+                out=acc[:], lhsT=w2_c[:, t, :].bitcast(FP4X4), lhsT_scale=w2_s[:, t, :],
                 rhs=og_w[:].bitcast(FP8X4), rhs_scale=og_s[:], start=True, stop=True,
             )
             nc.vector.tensor_copy(out=b[t][:], in_=acc[:])
@@ -168,31 +173,26 @@ def tile_picked_tokens_plain_two_bucketgap_store_endsteps_kernel(
         vg_w = tile("vg_w", [P, 2 * N], U8, "w_c")
         nc.vector.tensor_copy(out=vg_w[:].bitcast(U16), in_=vs_w[:].bitcast(U16).indirect(l5[:]))
 
-        pages = [zeroed(nc.gpsimd, "page%d" % i, [P, U], F32, ("w2_w", "w2_plane")[i]) for i in range(2)]
+        pages = [zeroed(nc.gpsimd, "page%d" % i, [P, U], F32, ("picked_scales", "w2_c")[i]) for i in range(2)]
         sums = tile("sums", [P, 4, O], F32, "picked_words")
-        for t in range(3):
+        for t in range(4):
             bucket_sums(t, 0, O)
 
-        picked = tile("picked", [P, 4, O], F32)
+        picked = [tile("picked%d" % h, [P, 4, HALF], F32, ("picked0", "board0")[h]) for h in range(2)]
         for h in range(2):
             o0 = h * HALF
-            cols = slice(o0, o0 + HALF)
-            bucket_sums(3, o0, HALF)
             for t in range(4):
                 nc.scalar.activation(
-                    out=picked[:, t, cols], in_=b[t][:].indirect(l4[:, o0 // 16 : (o0 + HALF) // 16]),
+                    out=picked[h][:, t, :], in_=b[t][:].indirect(l4[:, o0 // 16 : (o0 + HALF) // 16]),
                     func=COPY, scale=sa_t[:, t : t + 1],
                 )
         for h in range(2):
             o0 = h * HALF
             cols = slice(o0, o0 + HALF)
-            gap = tile("gap%d" % h, [P, 4, HALF], BF16, ("gap0", "hid0")[h])
-            nc.vector.tensor_tensor(out=gap[:, 0:3, :], in0=sums[:, 0:3, cols], in1=picked[:, 0:3, cols], op=ALU.subtract)
-            nc.vector.tensor_tensor(out=gap[:, 3, :], in0=sums[:, 3, cols], in1=picked[:, 3, cols], op=ALU.subtract)
-            size = tile("size%d" % h, [P, 4, HALF], BF16)
-            nc.vector.scalar_tensor_tensor(out=size[:], in0=gap[:], scalar=-1.0, in1=gap[:], op0=ALU.mult, op1=ALU.max)
+            gap = tile("gap%d" % h, [P, 4, HALF], F32)
+            nc.vector.tensor_tensor(out=gap[:], in0=sums[:, :, cols], in1=picked[h][:], op=ALU.subtract)
             hid = tile("hid%d" % h, [P, HALF, 4], BF16)
-            nc.vector.tensor_copy(out=hid[:], in_=size[:].rearrange("p t o -> p o t"))
+            nc.scalar.activation(out=hid[:], in_=gap[:].rearrange("p t o -> p o t"), func=ABS)
             hq_w = tile("hq_w%d" % h, [P, HALF], U32)
             hq_s = tile("hq_s%d" % h, [P, HALF], U8)
             nc.vector.quantize_mx(out=hq_w[:].bitcast(FP8X4), scales=hq_s[:], in_=hid[:].rearrange("p o t -> p (o t)"))

@@ -94,7 +94,7 @@ def tile_picked_tokens_plain_two_bucketgap_store_endsteps_kernel(
         w2_c = tile("w2_c", [P, 4, P], U16)
         nc.scalar.copy(out=w2_c[:], in_=w2_w[:].bitcast(U16).rearrange("p (m t) -> p t m", t=4))
         w_s0 = tile("w_s0", [P, P], U8)
-        w_s = tile("w_s", [P, 3, P], U8)
+        w_s = tile("w_s", [P, 3, P], U8, "xt_stage")
         nc.vector.tensor_copy(out=w_s0[:], in_=w_plane[:].rearrange("p (m t) -> p t m", t=4)[:, 0, :])
         w_c0 = tile("w_c0", [P, P], U32)
         w_c = tile("w_c", [P, 3, P], U32)
@@ -105,7 +105,7 @@ def tile_picked_tokens_plain_two_bucketgap_store_endsteps_kernel(
         rest_w = tile("rest_w", [P, J - HEAD], U32, "picked_words")
         nc.vector.tensor_copy(out=head_s[:], in_=xt_plane[:].indirect(l1[:, : HEAD // 16]))
         nc.vector.tensor_copy(out=head_w[:], in_=xt_w[:].bitcast(U32).indirect(l1[:, : HEAD // 16]))
-        nc.vector.tensor_copy(out=w_s[:], in_=w_plane[:].rearrange("p (m t) -> p t m", t=4)[:, 1:, :])
+        nc.gpsimd.tensor_copy(out=w_s[:], in_=w_plane[:].rearrange("p (m t) -> p t m", t=4)[:, 1:, :])
         board2 = zeroed(nc.gpsimd, "board2", [P, C], F32, "w_plane")
         boards.append(board2)
         nc.vector.tensor_copy(out=rest_w[:], in_=xt_w[:].bitcast(U32).indirect(l1[:, HEAD // 16 :]))
@@ -168,17 +168,21 @@ def tile_picked_tokens_plain_two_bucketgap_store_endsteps_kernel(
             )
             nc.vector.tensor_copy(out=b[t][:], in_=acc[:])
 
-        vg_s = tile("vg_s", [P, N], U8, "w_s")
+        vg_s = tile("vg_s", [P, N], U8, "xt_stage")
         nc.vector.tensor_copy(out=vg_s[:], in_=vs_plane[:].indirect(l5[:]))
         vg_w = tile("vg_w", [P, 2 * N], U8, "w_c")
         nc.vector.tensor_copy(out=vg_w[:].bitcast(U16), in_=vs_w[:].bitcast(U16).indirect(l5[:]))
 
-        pages = [zeroed(nc.gpsimd, "page%d" % i, [P, U], F32, ("picked_scales", "w2_c")[i]) for i in range(2)]
         sums = tile("sums", [P, 4, O], F32, "picked_words")
-        for t in range(4):
+        pairs = tile("pairs", [P, O, 2], F32, "w_s0")
+        quads = boards[0][:].rearrange("p (o c) -> p o c", c=4)
+        nc.gpsimd.tensor_tensor(out=pairs[:], in0=quads[:, :, 0:2], in1=quads[:, :, 2:4], op=ALU.add)
+        nc.gpsimd.tensor_tensor(out=sums[:, 0, :], in0=pairs[:, :, 0], in1=pairs[:, :, 1], op=ALU.add)
+        pages = [zeroed(nc.gpsimd, "page%d" % i, [P, U], F32, ("picked_scales", "w2_c")[i]) for i in range(2)]
+        for t in range(1, 4):
             bucket_sums(t, 0, O)
 
-        picked = [tile("picked%d" % h, [P, 4, HALF], F32, ("picked0", "board0")[h]) for h in range(2)]
+        picked = [tile("picked%d" % h, [P, 4, HALF], F32, ("picked0", "board1")[h]) for h in range(2)]
         for h in range(2):
             o0 = h * HALF
             for t in range(4):

from contextlib import ExitStack

import concourse.mybir as mybir

F32 = mybir.dt.float32
BF16 = mybir.dt.bfloat16
I32 = mybir.dt.int32
U32 = mybir.dt.uint32
U16 = mybir.dt.uint16
U8 = mybir.dt.uint8
FP8X4 = mybir.dt.float8_e4m3fn_x4
FP4X4 = mybir.dt.float4_e2m1fn_x4
ALU = mybir.AluOpType
COPY = mybir.ActivationFunctionType.Copy
ABS = mybir.ActivationFunctionType.Abs
AX = mybir.AxisListType.X

P = 128
J, R, T, C, O, N, U = 512, 512, 1024, 1024, 256, 256, 512
FLOPS = 2 * 512 * 512 * 512 * 2 + 2 * 512 * 256 * 256
HEAD = 128
HALF = 128


def tile_picked_tokens_plain_two_bucketgap_store_endsteps_kernel(
    tc, xt_words, xt_scales, w_words, w_scales, xo_words, xo_scales, w2_words, w2_scales, sa,
    vs_words, vs_scales, offs, offs2, offs3, offs4, offs5, offs6, out,
):
    nc = tc.nc
    with ExitStack() as ctx:
        sb = ctx.enter_context(tc.tile_pool(name="sb", bufs=1))
        ps = ctx.enter_context(tc.psum_pool(name="ps", bufs=8))

        def tile(name, shape, dtype, tag=None):
            return sb.tile(shape, dtype, name=name, tag=tag or name, align_bytes=64)

        def bank():
            return ps.tile([P, 512], F32, name="bank")

        def load_list(name, src):
            t = tile(name, list(src.shape), U16)
            nc.sync.dma_start(t[:], src)
            return t

        def load_scale_rows(queue, plane, src):
            rows = src[0].bitcast(I32)
            for q in range(4):
                queue.dma_start(plane[32 * q : 32 * q + 4, :].bitcast(I32), rows[4 * q : 4 * q + 4, :])

        def zeroed(engine, name, shape, dtype, tag=None):
            t = tile(name, shape, dtype, tag)
            if dtype == U8:
                engine.memset(t[:].bitcast(I32), 0)
            else:
                engine.memset(t[:], 0.0)
            return t

        xt_plane = zeroed(nc.vector, "xt_plane", [P, T], U8)
        w_plane = zeroed(nc.vector, "w_plane", [P, R], U8)
        boards = [zeroed(nc.vector, "board%d" % i, [P, C], F32) for i in range(2)]

        w_stage = tile("w_stage", [4, 4, R // 4], I32)
        nc.sync.dma_start(w_stage[:], w_scales[0].bitcast(I32).rearrange("(q i) n -> i q n", i=4))
        xt_stage = tile("xt_stage", [4, 4, T // 4], I32)
        nc.sync.dma_start(xt_stage[:], xt_scales[0].bitcast(I32).rearrange("(q i) n -> i q n", i=4))
        l1 = load_list("l1", offs)
        w2_w = tile("w2_w", [P, 2 * R], U8)
        nc.sync.dma_start(w2_w[:].bitcast(I32), w2_words[0].bitcast(I32))
        xt_w = tile("xt_w", [P, T], I32)
        nc.sync.dma_start(xt_w[:], xt_words[0].rearrange("p n t -> p (n t)").bitcast(I32))
        w_w = tile("w_w", [P, R], I32)
        nc.sync.dma_start(w_w[:], w_words[0].rearrange("p n t -> p (n t)").bitcast(I32))
        l3 = load_list("l3", offs3)

        xo_plane = zeroed(nc.gpsimd, "xo_plane", [P, T], U8)
        w2_plane = zeroed(nc.gpsimd, "w2_plane", [P, R], U8)

        l2 = load_list("l2", offs2)
        load_scale_rows(nc.sync, xo_plane, xo_scales)
        xo_w = tile("xo_w", [P, T], I32)
        nc.sync.dma_start(xo_w[:], xo_words[0].rearrange("p n t -> p (n t)").bitcast(I32))
        load_scale_rows(nc.sync, w2_plane, w2_scales)
        l5 = load_list("l5", offs5)
        vs_w = tile("vs_w", [P, 2 * T], U8)
        nc.sync.dma_start(vs_w[:].bitcast(I32), vs_words[0].bitcast(I32))
        sa_t = tile("sa_t", [P, 4], F32)
        nc.sync.dma_start(sa_t[:], sa.rearrange("(p t) o -> p (t o)", t=4))
        l4 = load_list("l4", offs4)
        l6 = load_list("l6", offs6)

        for plane, stage in ((w_plane, w_stage), (xt_plane, xt_stage)):
            for q in range(4):
                nc.vector.tensor_copy(out=plane[32 * q : 32 * q + 4, :].bitcast(I32), in_=stage[:, q, :])
        w2_c = tile("w2_c", [P, 4, P], U16)
        nc.scalar.copy(out=w2_c[:], in_=w2_w[:].bitcast(U16).rearrange("p (m t) -> p t m", t=4))
        w_s0 = tile("w_s0", [P, P], U8)
        w_s = tile("w_s", [P, 3, P], U8, "xt_stage")
        nc.vector.tensor_copy(out=w_s0[:], in_=w_plane[:].rearrange("p (m t) -> p t m", t=4)[:, 0, :])
        w_c0 = tile("w_c0", [P, P], U32)
        w_c = tile("w_c", [P, 3, P], U32)
        nc.scalar.copy(out=w_c0[:], in_=w_w[:].bitcast(U32).rearrange("p (m t) -> p t m", t=4)[:, 0, :])
        nc.scalar.copy(out=w_c[:], in_=w_w[:].bitcast(U32).rearrange("p (m t) -> p t m", t=4)[:, 1:, :])
        head_s = tile("head_s", [P, HEAD], U8, "picked_scales")
        head_w = tile("head_w", [P, HEAD], U32)
        rest_w = tile("rest_w", [P, J - HEAD], U32, "picked_words")
        nc.vector.tensor_copy(out=head_s[:], in_=xt_plane[:].indirect(l1[:, : HEAD // 16]))
        nc.vector.tensor_copy(out=head_w[:], in_=xt_w[:].bitcast(U32).indirect(l1[:, : HEAD // 16]))
        nc.gpsimd.tensor_copy(out=w_s[:], in_=w_plane[:].rearrange("p (m t) -> p t m", t=4)[:, 1:, :])
        board2 = zeroed(nc.gpsimd, "board2", [P, C], F32, "w_plane")
        boards.append(board2)
        nc.vector.tensor_copy(out=rest_w[:], in_=xt_w[:].bitcast(U32).indirect(l1[:, HEAD // 16 :]))

        def product_a(dst, t, words, scale):
            w_codes, w_bytes = (w_c0[:], w_s0[:]) if t == 0 else (w_c[:, t - 1, :], w_s[:, t - 1, :])
            nc.tensor.matmul_mx(
                out=dst, lhsT=w_codes.bitcast(FP8X4), lhsT_scale=w_bytes,
                rhs=words.bitcast(FP8X4), rhs_scale=scale, start=True, stop=True,
            )

        a = [tile("a%d" % t, [P, J], F32) for t in range(4)]
        for t in range(4):
            acc = bank()
            product_a(acc[:, :HEAD], t, head_w[:], head_s[:])
            if t < 3:
                nc.scalar.activation(out=a[t][:, :HEAD], in_=acc[:, :HEAD], func=COPY)
                nc.scalar.activation(out=boards[t][:].indirect(l3[:, : HEAD // 16]), in_=a[t][:, :HEAD], func=COPY)
        last_acc = acc
        rest_s = tile("rest_s", [P, J - HEAD], U8, "picked_scales")
        nc.vector.tensor_copy(out=rest_s[:], in_=xt_plane[:].indirect(l1[:, HEAD // 16 :]))
        for t in range(4):
            acc = bank() if t < 3 else last_acc
            j0 = HEAD if t < 3 else 0
            product_a(acc[:, HEAD : 2 * HEAD], t, rest_w[:, :HEAD], rest_s[:, :HEAD])
            product_a(acc[:, 2 * HEAD :], t, rest_w[:, HEAD:], rest_s[:, HEAD:])
            nc.vector.tensor_copy(out=a[t][:, j0:], in_=acc[:, j0:])

        boards.append(zeroed(nc.gpsimd, "board3", [P, C], F32, "xt_plane"))
        vs_plane = zeroed(nc.gpsimd, "vs_plane", [P, T], U8, "w_c0")
        load_scale_rows(nc.sync, vs_plane, vs_scales)
        og_s = tile("og_s", [P, J], U8, tag="picked_scales")
        nc.vector.tensor_copy(out=og_s[:], in_=xo_plane[:].indirect(l2[:]))
        og_w = tile("og_w", [P, J], U32, tag="picked_words")
        nc.vector.tensor_copy(out=og_w[:], in_=xo_w[:].bitcast(U32).indirect(l2[:]))
        w2_s = tile("w2_s", [P, 4, P], U8, "w_s0")
        nc.vector.tensor_copy(out=w2_s[:], in_=w2_plane[:].rearrange("p (m t) -> p t m", t=4))


        def scatter_a(t):
            j0 = HEAD if t < 3 else 0
            nc.scalar.activation(out=boards[t][:].indirect(l3[:, j0 // 16 :]), in_=a[t][:, j0:], func=COPY)

        def bucket_sums(t, o0, n):
            nc.vector.tensor_reduce(
                out=sums[:, t, o0 : o0 + n],
                in_=boards[t][:, 4 * o0 : 4 * (o0 + n)].rearrange("p (o c) -> p o c", c=4),
                axis=AX, op=ALU.add,
            )

        for t in range(4):
            scatter_a(t)

        b = [tile("b%d" % t, [P, J], F32) for t in range(4)]
        for t in range(4):
            acc = bank()
            nc.tensor.matmul_mx(
                out=acc[:], lhsT=w2_c[:, t, :].bitcast(FP4X4), lhsT_scale=w2_s[:, t, :],
                rhs=og_w[:].bitcast(FP8X4), rhs_scale=og_s[:], start=True, stop=True,
            )
            nc.vector.tensor_copy(out=b[t][:], in_=acc[:])

        vg_s = tile("vg_s", [P, N], U8, "xt_stage")
        nc.vector.tensor_copy(out=vg_s[:], in_=vs_plane[:].indirect(l5[:]))
        vg_w = tile("vg_w", [P, 2 * N], U8, "w_c")
        nc.vector.tensor_copy(out=vg_w[:].bitcast(U16), in_=vs_w[:].bitcast(U16).indirect(l5[:]))

        sums = tile("sums", [P, 4, O], F32, "picked_words")
        pairs = tile("pairs", [P, O, 2], F32, "w_s0")
        quads = boards[0][:].rearrange("p (o c) -> p o c", c=4)
        nc.gpsimd.tensor_tensor(out=pairs[:], in0=quads[:, :, 0:2], in1=quads[:, :, 2:4], op=ALU.add)
        nc.gpsimd.tensor_tensor(out=sums[:, 0, :], in0=pairs[:, :, 0], in1=pairs[:, :, 1], op=ALU.add)
        pages = [zeroed(nc.gpsimd, "page%d" % i, [P, U], F32, ("picked_scales", "w2_c")[i]) for i in range(2)]
        for t in range(1, 4):
            bucket_sums(t, 0, O)

        picked = [tile("picked%d" % h, [P, 4, HALF], F32, ("picked0", "board1")[h]) for h in range(2)]
        for h in range(2):
            o0 = h * HALF
            for t in range(4):
                nc.scalar.activation(
                    out=picked[h][:, t, :], in_=b[t][:].indirect(l4[:, o0 // 16 : (o0 + HALF) // 16]),
                    func=COPY, scale=sa_t[:, t : t + 1],
                )
        for h in range(2):
            o0 = h * HALF
            cols = slice(o0, o0 + HALF)
            gap = tile("gap%d" % h, [P, 4, HALF], F32)
            nc.vector.tensor_tensor(out=gap[:], in0=sums[:, :, cols], in1=picked[h][:], op=ALU.subtract)
            hid = tile("hid%d" % h, [P, HALF, 4], BF16)
            nc.scalar.activation(out=hid[:], in_=gap[:].rearrange("p t o -> p o t"), func=ABS)
            hq_w = tile("hq_w%d" % h, [P, HALF], U32)
            hq_s = tile("hq_s%d" % h, [P, HALF], U8)
            nc.vector.quantize_mx(out=hq_w[:].bitcast(FP8X4), scales=hq_s[:], in_=hid[:].rearrange("p o t -> p (o t)"))
            acc = bank()
            for n in range(2):
                nc.tensor.matmul_mx(
                    out=acc[:, n * HALF : (n + 1) * HALF],
                    lhsT=vg_w[:, 2 * P * n : 2 * P * (n + 1)].bitcast(FP4X4), lhsT_scale=vg_s[:, P * n : P * (n + 1)],
                    rhs=hq_w[:].bitcast(FP8X4), rhs_scale=hq_s[:], start=True, stop=True,
                )
            res = tile("res%d" % h, [P, 2 * HALF], F32)
            if h == 0:
                nc.scalar.copy(out=res[:], in_=acc[:, : 2 * HALF])
            else:
                nc.vector.tensor_copy(out=res[:], in_=acc[:, : 2 * HALF])
            for n in range(2):
                nc.scalar.activation(
                    out=pages[n][:].indirect(l6[:, o0 // 16 : (o0 + HALF) // 16]),
                    in_=res[:, n * HALF : (n + 1) * HALF], func=COPY,
                )
        for n in range(2):
            y = tile("y%d" % n, [P, U], F32)
            nc.vector.tensor_copy(out=y[:, 0:1], in_=pages[n][:, 0:1])
            nc.vector.tensor_tensor(out=y[:, 1:U // 2], in0=pages[n][:, 1:U // 2], in1=pages[n][:, 0:U // 2 - 1], op=ALU.subtract)
            nc.sync.dma_start(out[n * P : (n + 1) * P, : U // 2], y[:, : U // 2])
            nc.vector.tensor_tensor(out=y[:, U // 2 :], in0=pages[n][:, U // 2 :], in1=pages[n][:, U // 2 - 1 : U - 1], op=ALU.subtract)
            nc.sync.dma_start(out[n * P : (n + 1) * P, U // 2 :], y[:, U // 2 :])
